import numpy as np
import ml_dtypes


def mxq(x, axis, fmt="e4m3"):
    dtype, down = {"e4m3": (ml_dtypes.float8_e4m3fn, 7), "e5m2": (ml_dtypes.float8_e5m2, 14)}[fmt]
    v = np.moveaxis(np.asarray(x, np.float32).astype(ml_dtypes.bfloat16).astype(np.float64), axis, -1)
    blocks = v.reshape(v.shape[:-1] + (-1, 32))
    amax = np.abs(blocks).max(-1, keepdims=True)
    byte = np.maximum(np.where(amax > 0, np.frexp(amax)[1] - 1 + 127, 0) - down, 1)
    scale = np.exp2(byte - 127.0)
    codes = (blocks / scale).astype(np.float32).astype(dtype).astype(np.float64)
    return np.moveaxis((codes * scale).reshape(v.shape), -1, axis)


WIDE = False


def mx_kscale(k):
    if not WIDE:
        return np.ones(k)
    levels = np.array([10, -10, 5, -5, 0])
    if k % 512:
        return np.exp2(np.random.permutation(np.resize(levels, k // 32))).repeat(32)
    a = np.empty((k // 512, 16))
    for p in range(k // 512):
        a[p, :8] = np.random.permutation(np.resize(levels, 8))
        for g in range(8):
            far = levels[np.abs(levels - a[p, g]) >= 10]
            a[p, g + 8] = far[np.random.randint(len(far))]
    return np.exp2(a.ravel()).repeat(32)


def f64(x):
    return np.asarray(x).astype(np.float64)


def striped(idx):
    return np.tile(idx.reshape(-1, 16).T, (8, 1)).astype(np.uint16)


def unstriped(offs):
    return offs[:16].T.reshape(-1).astype(np.int64)


def striped8(idx):
    return np.concatenate([x.reshape(-1, 16).T for x in idx]).astype(np.uint16)


def runs(offs, k):
    lists = np.stack([offs[16 * r : 16 * r + 16].T.reshape(-1) for r in range(8)]).astype(np.int64)
    return lists[np.arange(k) % 512 // 64]


def pack_weight(w):
    k, n = w.shape
    w = f64(np.asarray(w, np.float32).astype(ml_dtypes.bfloat16)).reshape(k // 32, 32, n)
    amax = np.abs(w).max(1)
    byte = np.clip(np.where(amax > 0, np.frexp(amax)[1] - 1 + 127 - 7, 1), 1, 254)
    scaled = (w * np.exp2(127.0 - byte)[:, None, :]).reshape(k, n).astype(np.float32)
    words = np.ascontiguousarray(scaled.reshape(k // 512, 128, 4, n).transpose(0, 1, 3, 2)).astype(ml_dtypes.float8_e4m3fn).view(np.uint8)
    return words, np.ascontiguousarray(byte.astype(np.uint8).reshape(k // 512, 16, n))


def unpack_weight(words, scales):
    g, p, n, _ = words.shape
    vals = np.ascontiguousarray(words).view(ml_dtypes.float8_e4m3fn).astype(np.float64) * np.repeat(np.exp2(scales.astype(np.float64) - 127.0), 8, axis=1)[..., None]
    return vals.transpose(0, 1, 3, 2).reshape(g * 512, n)


def sigmoid(v):
    return 1.0 / (1.0 + np.exp(-np.maximum(v, -700.0)))

def planes(y):
    n, m = y.shape
    v = y.astype(np.float32).astype(ml_dtypes.bfloat16).astype(np.float64).reshape(n // 32, 32, m)
    top = np.abs(v).max(1)
    byte = np.clip(np.where(top > 0, np.frexp(top)[1] - 1 + 127 - 7, 1), 1, 254)
    codes = (v * np.exp2(127.0 - byte)[:, None, :]).reshape(n, m).astype(np.float32).astype(ml_dtypes.float8_e4m3fn).view(np.uint8)
    words = codes.reshape(n // 512, 128, 4, m).transpose(0, 1, 3, 2)
    return np.ascontiguousarray(words), np.ascontiguousarray(byte.astype(np.uint8).reshape(n // 512, 16, m))


K, T, S, N, H = 512, 2048, 512, 512, 512


def setup_inputs():
    n = np.random.standard_normal
    s = mx_kscale(K)[:, None]
    u = mx_kscale(H)
    packed_xT = pack_weight(n((K, T)) * s)
    packed_w1 = pack_weight(n((K, H)) / np.sqrt(K) / s)
    packed_w2 = pack_weight(n((H, N)) / np.sqrt(H) / u[:, None])
    return {
        "x_words": packed_xT[0],
        "x_scales": packed_xT[1],
        "w1_words": packed_w1[0],
        "w1_scales": packed_w1[1],
        "gn": (np.random.uniform(0.5, 1.5, (H, 1)) * u[:, None]).astype(np.float32),
        "w2_words": packed_w2[0],
        "w2_scales": packed_w2[1],
        "offs": striped(np.random.permutation(T)[:S]),
        "n1": striped8(np.stack([np.random.permutation(S) for _ in range(8)])),
        "n2": striped8(np.stack([np.random.permutation(S) for _ in range(8)])),
        "n3": striped8(np.stack([np.random.permutation(S) for _ in range(8)])),
    }


def reference(x_words, x_scales, w1_words, w1_scales, gn, w2_words, w2_scales, offs, n1, n2, n3):
    xq = unpack_weight(x_words, x_scales)[:, unstriped(offs)]
    y = unpack_weight(w1_words, w1_scales).T @ xq
    z = f64(gn) * (np.abs(y[np.arange(H)[:, None], runs(n1, H)] + y[np.arange(H)[:, None], runs(n2, H)] - y))
    h = unpack_weight(w2_words, w2_scales).T @ mxq(z, 0, "e4m3")
    a = h[np.arange(N)[:, None], runs(n3, N)]
    out_0 = sigmoid(a) * (h - a)
    return (out_0,) + planes(out_0)

@@ -1,0 +1,239 @@
+from contextlib import ExitStack
+
+import concourse.mybir as mybir
+
+F32 = mybir.dt.float32
+BF16 = mybir.dt.bfloat16
+I32 = mybir.dt.int32
+U32 = mybir.dt.uint32
+U16 = mybir.dt.uint16
+U8 = mybir.dt.uint8
+FP8X4 = mybir.dt.float8_e4m3fn_x4
+ALU = mybir.AluOpType
+ACT = mybir.ActivationFunctionType
+
+P = 128
+PACK = 4
+T = 2048
+S = 512
+QUADS = 4
+FLOPS = 2 * 2 * 512 * 512 * 512
+
+X_PIECES = ((0, 256), (256, 256))
+Z_PIECES = ((0, 256), (256, 128), (384, 128))
+OUT_PIECES = ((0, 256), (256, 128), (384, 128))
+
+
+def entries(lst, start, n):
+    return lst[:, start // 16 : (start + n) // 16]
+
+
+def tile_picked_absgate_none_po_kernel(
+    tc, x_words, x_scales, w1_words, w1_scales, gn, w2_words, w2_scales, offs, n1, n2, n3, out_0, out_1, out_2
+):
+    nc = tc.nc
+    with ExitStack() as ctx:
+        lists = ctx.enter_context(tc.tile_pool(name="lists", bufs=1))
+        sb = ctx.enter_context(tc.tile_pool(name="sb", bufs=1))
+        psum = ctx.enter_context(tc.psum_pool(name="psum", bufs=8))
+
+        def tile(shape, dtype, name, tag=""):
+            return sb.tile(shape, dtype, name=name, tag=tag, align_bytes=64)
+
+        def as_words(words):
+            return words[0].rearrange("p n t -> p (n t)").bitcast(I32)
+
+        def load_scale_rows(queue, plane, scales):
+            for q in range(QUADS):
+                queue.dma_start(
+                    out=plane[32 * q : 32 * q + 4, :].bitcast(I32), in_=scales[0, 4 * q : 4 * q + 4, :].bitcast(I32)
+                )
+
+        offs_t = lists.tile([P, S // 16], U16, name="offs_t")
+        n1_t = lists.tile([P, S // 16], U16, name="n1_t")
+        n2_t = lists.tile([P, S // 16], U16, name="n2_t")
+        n3_t = lists.tile([P, S // 16], U16, name="n3_t")
+
+        xw = tile([P, T], U32, "xw")
+        xs = tile([P, T], U8, "xs")
+        w1_raw = tile([P, S], U32, "w1_raw")
+        w2_raw = tile([P, S], U32, "w2_raw")
+        w1s_raw = tile([P, S], U8, "w1s_raw")
+        w2s_raw = tile([P, S], U8, "w2s_raw")
+        w1s = tile([P, S], U8, "w1s", "dealt_scales")
+        gain = tile([P, PACK], F32, "gain")
+
+        nc.gpsimd.memset(w1s_raw[:].bitcast(I32), 0)
+        nc.vector.memset(xs[:].bitcast(I32), 0)
+        nc.vector.memset(w1s[:].bitcast(I32), 0)
+        nc.gpsimd.dma_start(out=gain[:], in_=gn.rearrange("(p t) o -> p (t o)", t=PACK))
+        nc.gpsimd.memset(w2s_raw[:].bitcast(I32), 0)
+        nc.scalar.dma_start(out=xw[:].bitcast(I32), in_=as_words(x_words))
+        nc.scalar.dma_start(out=w1_raw[:].bitcast(I32), in_=as_words(w1_words))
+        nc.sync.dma_start(out=offs_t[:], in_=offs)
+        nc.sync.dma_start(out=w1s_raw[0:16, :].bitcast(I32), in_=w1_scales[0].bitcast(I32))
+        load_scale_rows(nc.sync, xs, x_scales)
+        nc.sync.dma_start(out=n1_t[:], in_=n1)
+        nc.sync.dma_start(out=n2_t[:], in_=n2)
+        nc.sync.dma_start(out=n3_t[:], in_=n3)
+        nc.sync.dma_start(out=w2_raw[:].bitcast(I32), in_=as_words(w2_words))
+        load_scale_rows(nc.gpsimd, w2s_raw, w2_scales)
+
+        widest = 16
+        signs = tile([P, widest * PACK], BF16, "signs")
+        nc.scalar.activation(
+            out=signs[:].rearrange("p (j t) -> p j t", t=PACK),
+            in_=gain[:].unsqueeze(1).to_broadcast([P, widest, PACK]),
+            func=ACT.Sign,
+        )
+
+        def dealt_view(t_major):
+            return t_major[:].rearrange("p (t c i) -> p c t i", t=PACK, i=4)
+
+        def raw_view(raw):
+            return raw[:].rearrange("p (c i t) -> p c t i", t=PACK, i=4)
+
+        w1s_rows = tile([P, S], U8, "w1s_rows")
+        nc.vector.tensor_copy(out=dealt_view(w1s_rows), in_=raw_view(w1s_raw))
+        for q in range(QUADS):
+            nc.scalar.dma_start(
+                out=w1s[32 * q : 32 * q + 4, :].bitcast(I32), in_=w1s_rows[4 * q : 4 * q + 4, :].bitcast(I32)
+            )
+
+        xs_g = tile([P, S], U8, "xs_g")
+        nc.vector.tensor_copy(out=xs_g[:], in_=xs[:].indirect(offs_t[:]))
+        xw_g = []
+        for h, (j0, n) in enumerate(X_PIECES):
+            g = tile([P, n], U32, f"xw_g{h}")
+            nc.vector.tensor_copy(out=g[:], in_=xw[:].indirect(entries(offs_t, j0, n)))
+            xw_g.append(g)
+
+        w1 = tile([P, S], U32, "w1", "dealt_words")
+        nc.scalar.copy(out=dealt_view(w1), in_=raw_view(w1_raw))
+
+        y = [tile([P, S], F32, f"y{t}") for t in range(PACK)]
+        y_acc = {}
+        for t in range(PACK):
+            for h, (j0, n) in enumerate(X_PIECES):
+                y_acc[t, h] = psum.tile([P, n], F32, name=f"y_acc{t}_{h}", tag="acc")
+                nc.tensor.matmul_mx(
+                    out=y_acc[t, h][:],
+                    lhsT=w1[:, t * P : (t + 1) * P].bitcast(FP8X4),
+                    lhsT_scale=w1s[:, t * P : (t + 1) * P],
+                    rhs=xw_g[h][:].bitcast(FP8X4),
+                    rhs_scale=xs_g[:, j0 : j0 + n],
+                    start=True,
+                    stop=True,
+                )
+
+        def y_out_of_psum(t):
+            for h, (j0, n) in enumerate(X_PIECES):
+                if t % 2:
+                    nc.vector.tensor_scalar(y[t][:, j0 : j0 + n], y_acc[t, h][:], gain[:, t : t + 1], None, ALU.mult)
+                else:
+                    nc.scalar.activation(
+                        out=y[t][:, j0 : j0 + n], in_=y_acc[t, h][:], func=ACT.Copy, scale=gain[:, t : t + 1]
+                    )
+
+        w2 = tile([P, S], U32, "w2", "dealt_words")
+        w2s = tile([P, S], U8, "w2s", "dealt_scales")
+        z_words = tile([P, S], U32, "z_words")
+        z_scales = tile([P, S], U8, "z_scales")
+        h_acc = []
+
+        def woven(flat):
+            return flat.rearrange("p (c i t) -> p c t i", t=PACK, i=4)
+
+        def planar(tile3):
+            return tile3[:].rearrange("p t (c i) -> p c t i", i=4)
+
+        for c, (j0, n) in enumerate(Z_PIECES):
+            first = tile([P, PACK, n], F32, f"first{c}")
+            both = tile([P, PACK, n], F32, f"both{c}")
+            diff = tile([P, PACK, n], F32, f"diff{c}")
+            for t in range(PACK + 1):
+                if t < PACK:
+                    if c == 0 and t % 2 == 0:
+                        y_out_of_psum(t)
+                        y_out_of_psum(t + 1)
+                    nc.scalar.activation(
+                        out=first[:, t, :], in_=y[t][:].indirect(entries(n1_t, j0, n)), func=ACT.Copy
+                    )
+                    nc.vector.tensor_tensor(
+                        both[:, t, :], y[t][:].indirect(entries(n2_t, j0, n)), first[:, t, :], ALU.add
+                    )
+                if t > 0:
+                    nc.vector.tensor_tensor(
+                        diff[:, t - 1, :], both[:, t - 1, :], y[t - 1][:, j0 : j0 + n], ALU.subtract
+                    )
+            if c == 0:
+                nc.scalar.copy(out=dealt_view(w2), in_=raw_view(w2_raw))
+                nc.gpsimd.tensor_copy(out=dealt_view(w2s), in_=raw_view(w2s_raw))
+                h_acc.extend(psum.tile([P, S], F32, name=f"h_acc{t}", tag="acc") for t in range(PACK))
+            size = tile([P, PACK * n], BF16, f"size{c}")
+            z = tile([P, PACK * n], BF16, f"z{c}")
+            nc.scalar.activation(out=woven(size[:]), in_=planar(diff), func=ACT.Abs)
+            nc.vector.tensor_tensor(
+                z[:].rearrange("p (r e) -> p r e", e=widest * PACK),
+                size[:].rearrange("p (r e) -> p r e", e=widest * PACK),
+                signs[:].unsqueeze(1).to_broadcast([P, n // widest, widest * PACK]),
+                ALU.mult,
+            )
+            nc.vector.quantize_mx(
+                out=z_words[:, j0 : j0 + n].bitcast(FP8X4), scales=z_scales[:, j0 : j0 + n], in_=z[:]
+            )
+            for t in range(PACK):
+                nc.tensor.matmul_mx(
+                    out=h_acc[t][:, j0 : j0 + n],
+                    lhsT=w2[:, t * P : (t + 1) * P].bitcast(FP8X4),
+                    lhsT_scale=w2s[:, t * P : (t + 1) * P],
+                    rhs=z_words[:, j0 : j0 + n].bitcast(FP8X4),
+                    rhs_scale=z_scales[:, j0 : j0 + n],
+                    start=True,
+                    stop=True,
+                )
+
+        half_h = [tile([P, S], F32, f"half_h{t}") for t in range(PACK)]
+        last0 = Z_PIECES[-1][0]
+        for j0, j1 in ((0, last0), (last0, S)):
+            for t in (0, 3, 1, 2):
+                if t >= 2:
+                    nc.vector.tensor_scalar(half_h[t][:, j0:j1], h_acc[t][:, j0:j1], 0.5, None, ALU.mult)
+                else:
+                    nc.scalar.activation(out=half_h[t][:, j0:j1], in_=h_acc[t][:, j0:j1], func=ACT.Copy, scale=0.5)
+
+        o_words = tile([P, S], U32, "o_words")
+        o_scales = tile([P, S], U8, "o_scales")
+        out_rows = out_0.rearrange("(p t) j -> p t j", t=PACK)
+        out_words = as_words(out_1)
+        for c, (j0, n) in enumerate(OUT_PIECES):
+            half_a = tile([P, PACK, n], F32, f"half_a{c}")
+            th = tile([P, PACK, n], F32, f"th{c}")
+            gap = tile([P, PACK, n], F32, f"gap{c}")
+            res = tile([P, PACK, n], F32, f"res{c}")
+            for t in (3, 0, 1, 2):
+                window = half_h[t][:].indirect(entries(n3_t, j0, n))
+                if t == 3 and c == 0:
+                    nc.vector.tensor_copy(out=half_a[:, t, :], in_=window)
+                else:
+                    nc.scalar.activation(out=half_a[:, t, :], in_=window, func=ACT.Copy)
+            for t in (3, 0, 1, 2):
+                nc.vector.tensor_tensor(gap[:, t, :], half_h[t][:, j0 : j0 + n], half_a[:, t, :], ALU.subtract)
+            for t0 in (0, 2):
+                nc.scalar.activation(out=th[:, t0 : t0 + 2, :], in_=half_a[:, t0 : t0 + 2, :], func=ACT.Tanh)
+            for t0 in (0, 2):
+                nc.vector.scalar_tensor_tensor(
+                    res[:, t0 : t0 + 2, :], th[:, t0 : t0 + 2, :], 1.0, gap[:, t0 : t0 + 2, :], ALU.add, ALU.mult
+                )
+            nc.sync.dma_start(out=out_rows[:, :, j0 : j0 + n], in_=res[:])
+            rounded = tile([P, PACK * n], BF16, f"rounded{c}")
+            nc.vector.tensor_copy(out=woven(rounded[:]), in_=planar(res))
+            nc.vector.quantize_mx(
+                out=o_words[:, j0 : j0 + n].bitcast(FP8X4), scales=o_scales[:, j0 : j0 + n], in_=rounded[:]
+            )
+            nc.sync.dma_start(out=out_words[:, j0 : j0 + n], in_=o_words[:, j0 : j0 + n].bitcast(I32))
+        for q in range(QUADS):
+            queue = nc.sync if q % 2 else nc.scalar
+            queue.dma_start(
+                out=out_2[0, 4 * q : 4 * q + 4, :].bitcast(I32), in_=o_scales[32 * q : 32 * q + 4, :].bitcast(I32)
+            )

@@ -43,8 +43,8 @@ def tile_picked_absgate_none_po_kernel(
         def as_words(words):
             return words[0].rearrange("p n t -> p (n t)").bitcast(I32)
 
-        def load_scale_rows(queue, plane, scales):
-            for q in range(QUADS):
+        def load_scale_rows(plane, scales, queues):
+            for q, queue in queues.items():
                 queue.dma_start(
                     out=plane[32 * q : 32 * q + 4, :].bitcast(I32), in_=scales[0, 4 * q : 4 * q + 4, :].bitcast(I32)
                 )
@@ -56,28 +56,27 @@ def tile_picked_absgate_none_po_kernel(
 
         xw = tile([P, T], U32, "xw")
         xs = tile([P, T], U8, "xs")
-        w1_raw = tile([P, S], U32, "w1_raw")
+        w_raw = tile([P, S], U32, "w_raw")
+        ws_raw = tile([P, S], U8, "ws_raw")
         w2_raw = tile([P, S], U32, "w2_raw")
-        w1s_raw = tile([P, S], U8, "w1s_raw")
         w2s_raw = tile([P, S], U8, "w2s_raw")
-        w1s = tile([P, S], U8, "w1s", "dealt_scales")
         gain = tile([P, PACK], F32, "gain")
 
-        nc.gpsimd.memset(w1s_raw[:].bitcast(I32), 0)
         nc.vector.memset(xs[:].bitcast(I32), 0)
-        nc.vector.memset(w1s[:].bitcast(I32), 0)
-        nc.gpsimd.dma_start(out=gain[:], in_=gn.rearrange("(p t) o -> p (t o)", t=PACK))
+        nc.gpsimd.memset(ws_raw[:].bitcast(I32), 0)
         nc.gpsimd.memset(w2s_raw[:].bitcast(I32), 0)
-        nc.scalar.dma_start(out=xw[:].bitcast(I32), in_=as_words(x_words))
-        nc.scalar.dma_start(out=w1_raw[:].bitcast(I32), in_=as_words(w1_words))
+        nc.gpsimd.dma_start(out=gain[:], in_=gn.rearrange("(p t) o -> p (t o)", t=PACK))
         nc.sync.dma_start(out=offs_t[:], in_=offs)
-        nc.sync.dma_start(out=w1s_raw[0:16, :].bitcast(I32), in_=w1_scales[0].bitcast(I32))
-        load_scale_rows(nc.sync, xs, x_scales)
+        load_scale_rows(ws_raw, w1_scales, {0: nc.sync, 1: nc.scalar})
+        load_scale_rows(xs, x_scales, {0: nc.scalar, 1: nc.scalar, 2: nc.sync, 3: nc.sync})
+        nc.sync.dma_start(out=xw[:].bitcast(I32), in_=as_words(x_words))
+        load_scale_rows(ws_raw, w1_scales, {2: nc.sync, 3: nc.sync})
+        nc.sync.dma_start(out=w_raw[:].bitcast(I32), in_=as_words(w1_words))
         nc.sync.dma_start(out=n1_t[:], in_=n1)
         nc.sync.dma_start(out=n2_t[:], in_=n2)
-        nc.sync.dma_start(out=n3_t[:], in_=n3)
+        load_scale_rows(w2s_raw, w2_scales, {q: nc.sync for q in range(QUADS)})
         nc.sync.dma_start(out=w2_raw[:].bitcast(I32), in_=as_words(w2_words))
-        load_scale_rows(nc.gpsimd, w2s_raw, w2_scales)
+        nc.sync.dma_start(out=n3_t[:], in_=n3)
 
         widest = 16
         signs = tile([P, widest * PACK], BF16, "signs")
@@ -93,23 +92,16 @@ def tile_picked_absgate_none_po_kernel(
         def raw_view(raw):
             return raw[:].rearrange("p (c i t) -> p c t i", t=PACK, i=4)
 
-        w1s_rows = tile([P, S], U8, "w1s_rows")
-        nc.vector.tensor_copy(out=dealt_view(w1s_rows), in_=raw_view(w1s_raw))
-        for q in range(QUADS):
-            nc.scalar.dma_start(
-                out=w1s[32 * q : 32 * q + 4, :].bitcast(I32), in_=w1s_rows[4 * q : 4 * q + 4, :].bitcast(I32)
-            )
-
         xs_g = tile([P, S], U8, "xs_g")
-        nc.vector.tensor_copy(out=xs_g[:], in_=xs[:].indirect(offs_t[:]))
-        xw_g = []
-        for h, (j0, n) in enumerate(X_PIECES):
-            g = tile([P, n], U32, f"xw_g{h}")
-            nc.vector.tensor_copy(out=g[:], in_=xw[:].indirect(entries(offs_t, j0, n)))
-            xw_g.append(g)
-
+        xw_g = [tile([P, n], U32, f"xw_g{h}") for h, (j0, n) in enumerate(X_PIECES)]
         w1 = tile([P, S], U32, "w1", "dealt_words")
-        nc.scalar.copy(out=dealt_view(w1), in_=raw_view(w1_raw))
+        w1s = tile([P, S], U8, "w1s", "dealt_scales")
+        for t0 in (0, 2):
+            nc.gpsimd.tensor_copy(out=dealt_view(w1s)[:, :, t0 : t0 + 2, :], in_=raw_view(ws_raw)[:, :, t0 : t0 + 2, :])
+            nc.scalar.copy(out=dealt_view(w1)[:, :, t0 : t0 + 2, :], in_=raw_view(w_raw)[:, :, t0 : t0 + 2, :])
+        nc.vector.tensor_copy(out=xs_g[:], in_=xs[:].indirect(offs_t[:]))
+        for h, (j0, n) in enumerate(X_PIECES):
+            nc.vector.tensor_copy(out=xw_g[h][:], in_=xw[:].indirect(entries(offs_t, j0, n)))
 
         y = [tile([P, S], F32, f"y{t}") for t in range(PACK)]
         y_acc = {}
@@ -128,7 +120,7 @@ def tile_picked_absgate_none_po_kernel(
 
         def y_out_of_psum(t):
             for h, (j0, n) in enumerate(X_PIECES):
-                if t % 2:
+                if t in (1, 2):
                     nc.vector.tensor_scalar(y[t][:, j0 : j0 + n], y_acc[t, h][:], gain[:, t : t + 1], None, ALU.mult)
                 else:
                     nc.scalar.activation(
@@ -139,7 +131,7 @@ def tile_picked_absgate_none_po_kernel(
         w2s = tile([P, S], U8, "w2s", "dealt_scales")
         z_words = tile([P, S], U32, "z_words")
         z_scales = tile([P, S], U8, "z_scales")
-        h_acc = []
+        h_acc = {}
 
         def woven(flat):
             return flat.rearrange("p (c i t) -> p c t i", t=PACK, i=4)
@@ -148,9 +140,9 @@ def tile_picked_absgate_none_po_kernel(
             return tile3[:].rearrange("p t (c i) -> p c t i", i=4)
 
         for c, (j0, n) in enumerate(Z_PIECES):
-            first = tile([P, PACK, n], F32, f"first{c}")
+            first = tile([P, PACK, n], F32, f"first{c}", "")
             both = tile([P, PACK, n], F32, f"both{c}")
-            diff = tile([P, PACK, n], F32, f"diff{c}")
+            diff = tile([P, PACK, n], F32, f"diff{c}", f"diff{c}")
             for t in range(PACK + 1):
                 if t < PACK:
                     if c == 0 and t % 2 == 0:
@@ -168,8 +160,7 @@ def tile_picked_absgate_none_po_kernel(
                     )
             if c == 0:
                 nc.scalar.copy(out=dealt_view(w2), in_=raw_view(w2_raw))
-                nc.gpsimd.tensor_copy(out=dealt_view(w2s), in_=raw_view(w2s_raw))
-                h_acc.extend(psum.tile([P, S], F32, name=f"h_acc{t}", tag="acc") for t in range(PACK))
+                nc.vector.tensor_copy(out=dealt_view(w2s), in_=raw_view(w2s_raw))
             size = tile([P, PACK * n], BF16, f"size{c}")
             z = tile([P, PACK * n], BF16, f"z{c}")
             nc.scalar.activation(out=woven(size[:]), in_=planar(diff), func=ACT.Abs)
@@ -183,8 +174,9 @@ def tile_picked_absgate_none_po_kernel(
                 out=z_words[:, j0 : j0 + n].bitcast(FP8X4), scales=z_scales[:, j0 : j0 + n], in_=z[:]
             )
             for t in range(PACK):
+                h_acc[c, t] = psum.tile([P, n], F32, name=f"h_acc{c}_{t}", tag="acc")
                 nc.tensor.matmul_mx(
-                    out=h_acc[t][:, j0 : j0 + n],
+                    out=h_acc[c, t][:],
                     lhsT=w2[:, t * P : (t + 1) * P].bitcast(FP8X4),
                     lhsT_scale=w2s[:, t * P : (t + 1) * P],
                     rhs=z_words[:, j0 : j0 + n].bitcast(FP8X4),
@@ -194,13 +186,12 @@ def tile_picked_absgate_none_po_kernel(
                 )
 
         half_h = [tile([P, S], F32, f"half_h{t}") for t in range(PACK)]
-        last0 = Z_PIECES[-1][0]
-        for j0, j1 in ((0, last0), (last0, S)):
-            for t in (0, 3, 1, 2):
-                if t >= 2:
-                    nc.vector.tensor_scalar(half_h[t][:, j0:j1], h_acc[t][:, j0:j1], 0.5, None, ALU.mult)
+        for c, (j0, n) in enumerate(Z_PIECES):
+            for t in range(PACK):
+                if t % 2 and c == len(Z_PIECES) - 1:
+                    nc.vector.tensor_scalar(half_h[t][:, j0 : j0 + n], h_acc[c, t][:], 0.5, None, ALU.mult)
                 else:
-                    nc.scalar.activation(out=half_h[t][:, j0:j1], in_=h_acc[t][:, j0:j1], func=ACT.Copy, scale=0.5)
+                    nc.scalar.activation(out=half_h[t][:, j0 : j0 + n], in_=h_acc[c, t][:], func=ACT.Copy, scale=0.5)
 
         o_words = tile([P, S], U32, "o_words")
         o_scales = tile([P, S], U8, "o_scales")
@@ -211,13 +202,13 @@ def tile_picked_absgate_none_po_kernel(
             th = tile([P, PACK, n], F32, f"th{c}")
             gap = tile([P, PACK, n], F32, f"gap{c}")
             res = tile([P, PACK, n], F32, f"res{c}")
-            for t in (3, 0, 1, 2):
+            for t in range(PACK):
                 window = half_h[t][:].indirect(entries(n3_t, j0, n))
-                if t == 3 and c == 0:
+                if t % 2 and c == 0:
                     nc.vector.tensor_copy(out=half_a[:, t, :], in_=window)
                 else:
                     nc.scalar.activation(out=half_a[:, t, :], in_=window, func=ACT.Copy)
-            for t in (3, 0, 1, 2):
+            for t in range(PACK):
                 nc.vector.tensor_tensor(gap[:, t, :], half_h[t][:, j0 : j0 + n], half_a[:, t, :], ALU.subtract)
             for t0 in (0, 2):
                 nc.scalar.activation(out=th[:, t0 : t0 + 2, :], in_=half_a[:, t0 : t0 + 2, :], func=ACT.Tanh)
@@ -227,7 +218,10 @@ def tile_picked_absgate_none_po_kernel(
                 )
             nc.sync.dma_start(out=out_rows[:, :, j0 : j0 + n], in_=res[:])
             rounded = tile([P, PACK * n], BF16, f"rounded{c}")
-            nc.vector.tensor_copy(out=woven(rounded[:]), in_=planar(res))
+            if c == 1:
+                nc.scalar.copy(out=woven(rounded[:]), in_=planar(res))
+            else:
+                nc.vector.tensor_copy(out=woven(rounded[:]), in_=planar(res))
             nc.vector.quantize_mx(
                 out=o_words[:, j0 : j0 + n].bitcast(FP8X4), scales=o_scales[:, j0 : j0 + n], in_=rounded[:]
             )

@@ -120,7 +120,7 @@ def tile_picked_absgate_none_po_kernel(
 
         def y_out_of_psum(t):
             for h, (j0, n) in enumerate(X_PIECES):
-                if t in (1, 2):
+                if t >= 2:
                     nc.vector.tensor_scalar(y[t][:, j0 : j0 + n], y_acc[t, h][:], gain[:, t : t + 1], None, ALU.mult)
                 else:
                     nc.scalar.activation(
@@ -139,10 +139,16 @@ def tile_picked_absgate_none_po_kernel(
         def planar(tile3):
             return tile3[:].rearrange("p t (c i) -> p c t i", i=4)
 
-        for c, (j0, n) in enumerate(Z_PIECES):
-            first = tile([P, PACK, n], F32, f"first{c}", "")
+        diffs = {}
+
+        def look_up(c):
+            j0, n = Z_PIECES[c]
+            first = tile([P, PACK, n], F32, f"first{c}")
             both = tile([P, PACK, n], F32, f"both{c}")
-            diff = tile([P, PACK, n], F32, f"diff{c}", f"diff{c}")
+            diffs[c] = tile([P, PACK, n], F32, f"diff{c}")
+            last = c == len(Z_PIECES) - 1
+            if last:
+                second = tile([P, PACK, n], F32, "second")
             for t in range(PACK + 1):
                 if t < PACK:
                     if c == 0 and t % 2 == 0:
@@ -151,19 +157,21 @@ def tile_picked_absgate_none_po_kernel(
                     nc.scalar.activation(
                         out=first[:, t, :], in_=y[t][:].indirect(entries(n1_t, j0, n)), func=ACT.Copy
                     )
-                    nc.vector.tensor_tensor(
-                        both[:, t, :], y[t][:].indirect(entries(n2_t, j0, n)), first[:, t, :], ALU.add
-                    )
+                    at_n2 = y[t][:].indirect(entries(n2_t, j0, n))
+                    if last and t >= 2:
+                        nc.scalar.activation(out=second[:, t, :], in_=at_n2, func=ACT.Copy)
+                        at_n2 = second[:, t, :]
+                    nc.vector.tensor_tensor(both[:, t, :], at_n2, first[:, t, :], ALU.add)
                 if t > 0:
                     nc.vector.tensor_tensor(
-                        diff[:, t - 1, :], both[:, t - 1, :], y[t - 1][:, j0 : j0 + n], ALU.subtract
+                        diffs[c][:, t - 1, :], both[:, t - 1, :], y[t - 1][:, j0 : j0 + n], ALU.subtract
                     )
-            if c == 0:
-                nc.scalar.copy(out=dealt_view(w2), in_=raw_view(w2_raw))
-                nc.vector.tensor_copy(out=dealt_view(w2s), in_=raw_view(w2s_raw))
+
+        def second_product(c):
+            j0, n = Z_PIECES[c]
             size = tile([P, PACK * n], BF16, f"size{c}")
             z = tile([P, PACK * n], BF16, f"z{c}")
-            nc.scalar.activation(out=woven(size[:]), in_=planar(diff), func=ACT.Abs)
+            nc.scalar.activation(out=woven(size[:]), in_=planar(diffs[c]), func=ACT.Abs)
             nc.vector.tensor_tensor(
                 z[:].rearrange("p (r e) -> p r e", e=widest * PACK),
                 size[:].rearrange("p (r e) -> p r e", e=widest * PACK),
@@ -184,6 +192,15 @@ def tile_picked_absgate_none_po_kernel(
                     start=True,
                     stop=True,
                 )
+
+        for c in range(len(Z_PIECES) + 1):
+            if c < len(Z_PIECES):
+                look_up(c)
+            if c == 0:
+                nc.scalar.copy(out=dealt_view(w2), in_=raw_view(w2_raw))
+                nc.vector.tensor_copy(out=dealt_view(w2s), in_=raw_view(w2s_raw))
+            else:
+                second_product(c - 1)
 
         half_h = [tile([P, S], F32, f"half_h{t}") for t in range(PACK)]
         for c, (j0, n) in enumerate(Z_PIECES):

@@ -193,19 +193,18 @@ def tile_picked_absgate_none_po_kernel(
                     stop=True,
                 )
 
-        for c in range(len(Z_PIECES) + 1):
-            if c < len(Z_PIECES):
-                look_up(c)
+        for c in range(len(Z_PIECES)):
+            look_up(c)
             if c == 0:
                 nc.scalar.copy(out=dealt_view(w2), in_=raw_view(w2_raw))
                 nc.vector.tensor_copy(out=dealt_view(w2s), in_=raw_view(w2s_raw))
-            else:
-                second_product(c - 1)
+        for c in range(len(Z_PIECES)):
+            second_product(c)
 
         half_h = [tile([P, S], F32, f"half_h{t}") for t in range(PACK)]
         for c, (j0, n) in enumerate(Z_PIECES):
             for t in range(PACK):
-                if t % 2 and c == len(Z_PIECES) - 1:
+                if t % 2:
                     nc.vector.tensor_scalar(half_h[t][:, j0 : j0 + n], h_acc[c, t][:], 0.5, None, ALU.mult)
                 else:
                     nc.scalar.activation(out=half_h[t][:, j0 : j0 + n], in_=h_acc[c, t][:], func=ACT.Copy, scale=0.5)

from contextlib import ExitStack

import concourse.mybir as mybir

F32 = mybir.dt.float32
BF16 = mybir.dt.bfloat16
I32 = mybir.dt.int32
U32 = mybir.dt.uint32
U16 = mybir.dt.uint16
U8 = mybir.dt.uint8
FP8X4 = mybir.dt.float8_e4m3fn_x4
ALU = mybir.AluOpType
ACT = mybir.ActivationFunctionType

P = 128
PACK = 4
T = 2048
S = 512
QUADS = 4
FLOPS = 2 * 2 * 512 * 512 * 512

X_PIECES = ((0, 256), (256, 256))
Z_PIECES = ((0, 256), (256, 128), (384, 128))
OUT_PIECES = ((0, 256), (256, 128), (384, 128))


def entries(lst, start, n):
    return lst[:, start // 16 : (start + n) // 16]


def tile_picked_absgate_none_po_kernel(
    tc, x_words, x_scales, w1_words, w1_scales, gn, w2_words, w2_scales, offs, n1, n2, n3, out_0, out_1, out_2
):
    nc = tc.nc
    with ExitStack() as ctx:
        lists = ctx.enter_context(tc.tile_pool(name="lists", bufs=1))
        sb = ctx.enter_context(tc.tile_pool(name="sb", bufs=1))
        psum = ctx.enter_context(tc.psum_pool(name="psum", bufs=8))

        def tile(shape, dtype, name, tag=""):
            return sb.tile(shape, dtype, name=name, tag=tag, align_bytes=64)

        def as_words(words):
            return words[0].rearrange("p n t -> p (n t)").bitcast(I32)

        def load_scale_rows(plane, scales, queues):
            for q, queue in queues.items():
                queue.dma_start(
                    out=plane[32 * q : 32 * q + 4, :].bitcast(I32), in_=scales[0, 4 * q : 4 * q + 4, :].bitcast(I32)
                )

        offs_t = lists.tile([P, S // 16], U16, name="offs_t")
        n1_t = lists.tile([P, S // 16], U16, name="n1_t")
        n2_t = lists.tile([P, S // 16], U16, name="n2_t")
        n3_t = lists.tile([P, S // 16], U16, name="n3_t")

        xw = tile([P, T], U32, "xw")
        xs = tile([P, T], U8, "xs")
        w_raw = tile([P, S], U32, "w_raw")
        ws_raw = tile([P, S], U8, "ws_raw")
        w2_raw = tile([P, S], U32, "w2_raw")
        w2s_raw = tile([P, S], U8, "w2s_raw")
        gain = tile([P, PACK], F32, "gain")

        nc.vector.memset(xs[:].bitcast(I32), 0)
        nc.gpsimd.memset(ws_raw[:].bitcast(I32), 0)
        nc.gpsimd.memset(w2s_raw[:].bitcast(I32), 0)
        nc.gpsimd.dma_start(out=gain[:], in_=gn.rearrange("(p t) o -> p (t o)", t=PACK))
        nc.sync.dma_start(out=offs_t[:], in_=offs)
        load_scale_rows(ws_raw, w1_scales, {0: nc.sync, 1: nc.scalar})
        load_scale_rows(xs, x_scales, {0: nc.scalar, 1: nc.scalar, 2: nc.sync, 3: nc.sync})
        nc.sync.dma_start(out=xw[:].bitcast(I32), in_=as_words(x_words))
        load_scale_rows(ws_raw, w1_scales, {2: nc.sync, 3: nc.sync})
        nc.sync.dma_start(out=w_raw[:].bitcast(I32), in_=as_words(w1_words))
        nc.sync.dma_start(out=n1_t[:], in_=n1)
        nc.sync.dma_start(out=n2_t[:], in_=n2)
        load_scale_rows(w2s_raw, w2_scales, {q: nc.sync for q in range(QUADS)})
        nc.sync.dma_start(out=w2_raw[:].bitcast(I32), in_=as_words(w2_words))
        nc.sync.dma_start(out=n3_t[:], in_=n3)

        widest = 16
        signs = tile([P, widest * PACK], BF16, "signs")
        nc.scalar.activation(
            out=signs[:].rearrange("p (j t) -> p j t", t=PACK),
            in_=gain[:].unsqueeze(1).to_broadcast([P, widest, PACK]),
            func=ACT.Sign,
        )

        def dealt_view(t_major):
            return t_major[:].rearrange("p (t c i) -> p c t i", t=PACK, i=4)

        def raw_view(raw):
            return raw[:].rearrange("p (c i t) -> p c t i", t=PACK, i=4)

        xs_g = tile([P, S], U8, "xs_g")
        xw_g = [tile([P, n], U32, f"xw_g{h}") for h, (j0, n) in enumerate(X_PIECES)]
        w1 = tile([P, S], U32, "w1", "dealt_words")
        w1s = tile([P, S], U8, "w1s", "dealt_scales")
        for t0 in (0, 2):
            nc.gpsimd.tensor_copy(out=dealt_view(w1s)[:, :, t0 : t0 + 2, :], in_=raw_view(ws_raw)[:, :, t0 : t0 + 2, :])
            nc.scalar.copy(out=dealt_view(w1)[:, :, t0 : t0 + 2, :], in_=raw_view(w_raw)[:, :, t0 : t0 + 2, :])
        nc.vector.tensor_copy(out=xs_g[:], in_=xs[:].indirect(offs_t[:]))
        for h, (j0, n) in enumerate(X_PIECES):
            nc.vector.tensor_copy(out=xw_g[h][:], in_=xw[:].indirect(entries(offs_t, j0, n)))

        y = [tile([P, S], F32, f"y{t}") for t in range(PACK)]
        y_acc = {}
        for t in range(PACK):
            for h, (j0, n) in enumerate(X_PIECES):
                y_acc[t, h] = psum.tile([P, n], F32, name=f"y_acc{t}_{h}", tag="acc")
                nc.tensor.matmul_mx(
                    out=y_acc[t, h][:],
                    lhsT=w1[:, t * P : (t + 1) * P].bitcast(FP8X4),
                    lhsT_scale=w1s[:, t * P : (t + 1) * P],
                    rhs=xw_g[h][:].bitcast(FP8X4),
                    rhs_scale=xs_g[:, j0 : j0 + n],
                    start=True,
                    stop=True,
                )

        def y_out_of_psum(t):
            for h, (j0, n) in enumerate(X_PIECES):
                if t >= 2:
                    nc.vector.tensor_scalar(y[t][:, j0 : j0 + n], y_acc[t, h][:], gain[:, t : t + 1], None, ALU.mult)
                else:
                    nc.scalar.activation(
                        out=y[t][:, j0 : j0 + n], in_=y_acc[t, h][:], func=ACT.Copy, scale=gain[:, t : t + 1]
                    )

        w2 = tile([P, S], U32, "w2", "dealt_words")
        w2s = tile([P, S], U8, "w2s", "dealt_scales")
        z_words = tile([P, S], U32, "z_words")
        z_scales = tile([P, S], U8, "z_scales")
        h_acc = {}

        def woven(flat):
            return flat.rearrange("p (c i t) -> p c t i", t=PACK, i=4)

        def planar(tile3):
            return tile3[:].rearrange("p t (c i) -> p c t i", i=4)

        diffs = {}

        def look_up(c):
            j0, n = Z_PIECES[c]
            first = tile([P, PACK, n], F32, f"first{c}")
            both = tile([P, PACK, n], F32, f"both{c}")
            diffs[c] = tile([P, PACK, n], F32, f"diff{c}")
            last = c == len(Z_PIECES) - 1
            if last:
                second = tile([P, PACK, n], F32, "second")
            for t in range(PACK + 1):
                if t < PACK:
                    if c == 0 and t % 2 == 0:
                        y_out_of_psum(t)
                        y_out_of_psum(t + 1)
                    nc.scalar.activation(
                        out=first[:, t, :], in_=y[t][:].indirect(entries(n1_t, j0, n)), func=ACT.Copy
                    )
                    at_n2 = y[t][:].indirect(entries(n2_t, j0, n))
                    if last and t >= 2:
                        nc.scalar.activation(out=second[:, t, :], in_=at_n2, func=ACT.Copy)
                        at_n2 = second[:, t, :]
                    nc.vector.tensor_tensor(both[:, t, :], at_n2, first[:, t, :], ALU.add)
                if t > 0:
                    nc.vector.tensor_tensor(
                        diffs[c][:, t - 1, :], both[:, t - 1, :], y[t - 1][:, j0 : j0 + n], ALU.subtract
                    )

        def second_product(c):
            j0, n = Z_PIECES[c]
            size = tile([P, PACK * n], BF16, f"size{c}")
            z = tile([P, PACK * n], BF16, f"z{c}")
            nc.scalar.activation(out=woven(size[:]), in_=planar(diffs[c]), func=ACT.Abs)
            nc.vector.tensor_tensor(
                z[:].rearrange("p (r e) -> p r e", e=widest * PACK),
                size[:].rearrange("p (r e) -> p r e", e=widest * PACK),
                signs[:].unsqueeze(1).to_broadcast([P, n // widest, widest * PACK]),
                ALU.mult,
            )
            nc.vector.quantize_mx(
                out=z_words[:, j0 : j0 + n].bitcast(FP8X4), scales=z_scales[:, j0 : j0 + n], in_=z[:]
            )
            for t in range(PACK):
                h_acc[c, t] = psum.tile([P, n], F32, name=f"h_acc{c}_{t}", tag="acc")
                nc.tensor.matmul_mx(
                    out=h_acc[c, t][:],
                    lhsT=w2[:, t * P : (t + 1) * P].bitcast(FP8X4),
                    lhsT_scale=w2s[:, t * P : (t + 1) * P],
                    rhs=z_words[:, j0 : j0 + n].bitcast(FP8X4),
                    rhs_scale=z_scales[:, j0 : j0 + n],
                    start=True,
                    stop=True,
                )

        for c in range(len(Z_PIECES)):
            look_up(c)
            if c == 0:
                nc.scalar.copy(out=dealt_view(w2), in_=raw_view(w2_raw))
                nc.vector.tensor_copy(out=dealt_view(w2s), in_=raw_view(w2s_raw))
        for c in range(len(Z_PIECES)):
            second_product(c)

        half_h = [tile([P, S], F32, f"half_h{t}") for t in range(PACK)]
        for c, (j0, n) in enumerate(Z_PIECES):
            for t in range(PACK):
                if t % 2:
                    nc.vector.tensor_scalar(half_h[t][:, j0 : j0 + n], h_acc[c, t][:], 0.5, None, ALU.mult)
                else:
                    nc.scalar.activation(out=half_h[t][:, j0 : j0 + n], in_=h_acc[c, t][:], func=ACT.Copy, scale=0.5)

        o_words = tile([P, S], U32, "o_words")
        o_scales = tile([P, S], U8, "o_scales")
        out_rows = out_0.rearrange("(p t) j -> p t j", t=PACK)
        out_words = as_words(out_1)
        for c, (j0, n) in enumerate(OUT_PIECES):
            half_a = tile([P, PACK, n], F32, f"half_a{c}")
            th = tile([P, PACK, n], F32, f"th{c}")
            gap = tile([P, PACK, n], F32, f"gap{c}")
            res = tile([P, PACK, n], F32, f"res{c}")
            for t in range(PACK):
                window = half_h[t][:].indirect(entries(n3_t, j0, n))
                if t % 2 and c == 0:
                    nc.vector.tensor_copy(out=half_a[:, t, :], in_=window)
                else:
                    nc.scalar.activation(out=half_a[:, t, :], in_=window, func=ACT.Copy)
            for t in range(PACK):
                nc.vector.tensor_tensor(gap[:, t, :], half_h[t][:, j0 : j0 + n], half_a[:, t, :], ALU.subtract)
            for t0 in (0, 2):
                nc.scalar.activation(out=th[:, t0 : t0 + 2, :], in_=half_a[:, t0 : t0 + 2, :], func=ACT.Tanh)
            for t0 in (0, 2):
                nc.vector.scalar_tensor_tensor(
                    res[:, t0 : t0 + 2, :], th[:, t0 : t0 + 2, :], 1.0, gap[:, t0 : t0 + 2, :], ALU.add, ALU.mult
                )
            nc.sync.dma_start(out=out_rows[:, :, j0 : j0 + n], in_=res[:])
            rounded = tile([P, PACK * n], BF16, f"rounded{c}")
            if c == 1:
                nc.scalar.copy(out=woven(rounded[:]), in_=planar(res))
            else:
                nc.vector.tensor_copy(out=woven(rounded[:]), in_=planar(res))
            nc.vector.quantize_mx(
                out=o_words[:, j0 : j0 + n].bitcast(FP8X4), scales=o_scales[:, j0 : j0 + n], in_=rounded[:]
            )
            nc.sync.dma_start(out=out_words[:, j0 : j0 + n], in_=o_words[:, j0 : j0 + n].bitcast(I32))
        for q in range(QUADS):
            queue = nc.sync if q % 2 else nc.scalar
            queue.dma_start(
                out=out_2[0, 4 * q : 4 * q + 4, :].bitcast(I32), in_=o_scales[32 * q : 32 * q + 4, :].bitcast(I32)
            )
